import numpy as np
import ml_dtypes


def mxq(x, axis, fmt="e4m3"):
    dtype, down = {"e4m3": (ml_dtypes.float8_e4m3fn, 7), "e5m2": (ml_dtypes.float8_e5m2, 14)}[fmt]
    v = np.moveaxis(np.asarray(x, np.float32).astype(ml_dtypes.bfloat16).astype(np.float64), axis, -1)
    blocks = v.reshape(v.shape[:-1] + (-1, 32))
    amax = np.abs(blocks).max(-1, keepdims=True)
    byte = np.maximum(np.where(amax > 0, np.frexp(amax)[1] - 1 + 127, 0) - down, 1)
    scale = np.exp2(byte - 127.0)
    codes = (blocks / scale).astype(np.float32).astype(dtype).astype(np.float64)
    return np.moveaxis((codes * scale).reshape(v.shape), -1, axis)


WIDE = False


def mx_kscale(k):
    if not WIDE:
        return np.ones(k)
    levels = np.array([10, -10, 5, -5, 0])
    if k % 512:
        return np.exp2(np.random.permutation(np.resize(levels, k // 32))).repeat(32)
    a = np.empty((k // 512, 16))
    for p in range(k // 512):
        a[p, :8] = np.random.permutation(np.resize(levels, 8))
        for g in range(8):
            far = levels[np.abs(levels - a[p, g]) >= 10]
            a[p, g + 8] = far[np.random.randint(len(far))]
    return np.exp2(a.ravel()).repeat(32)


def f64(x):
    return np.asarray(x).astype(np.float64)


def striped(idx):
    return np.tile(idx.reshape(-1, 16).T, (8, 1)).astype(np.uint16)


def unstriped(offs):
    return offs[:16].T.reshape(-1).astype(np.int64)


def striped8(idx):
    return np.concatenate([x.reshape(-1, 16).T for x in idx]).astype(np.uint16)


def runs(offs, k):
    lists = np.stack([offs[16 * r : 16 * r + 16].T.reshape(-1) for r in range(8)]).astype(np.int64)
    return lists[np.arange(k) % 512 // 64]


def pack_weight(w):
    k, n = w.shape
    w = f64(np.asarray(w, np.float32).astype(ml_dtypes.bfloat16)).reshape(k // 32, 32, n)
    amax = np.abs(w).max(1)
    byte = np.clip(np.where(amax > 0, np.frexp(amax)[1] - 1 + 127 - 7, 1), 1, 254)
    scaled = (w * np.exp2(127.0 - byte)[:, None, :]).reshape(k, n).astype(np.float32)
    words = np.ascontiguousarray(scaled.reshape(k // 512, 128, 4, n).transpose(0, 1, 3, 2)).astype(ml_dtypes.float8_e4m3fn).view(np.uint8)
    return words, np.ascontiguousarray(byte.astype(np.uint8).reshape(k // 512, 16, n))


def unpack_weight(words, scales):
    g, p, n, _ = words.shape
    vals = np.ascontiguousarray(words).view(ml_dtypes.float8_e4m3fn).astype(np.float64) * np.repeat(np.exp2(scales.astype(np.float64) - 127.0), 8, axis=1)[..., None]
    return vals.transpose(0, 1, 3, 2).reshape(g * 512, n)


def sigmoid(v):
    return 1.0 / (1.0 + np.exp(-np.maximum(v, -700.0)))


K, T, S, H, W, C, G = 512, 1024, 512, 512, 2048, 512, 2048


def setup_inputs():
    n = np.random.standard_normal
    s = mx_kscale(K)[:, None]
    packed_xT = pack_weight(n((K, T)) * s)
    packed_dT = pack_weight(n((K, G)) / s)
    return {
        "x_words": packed_xT[0],
        "x_scales": packed_xT[1],
        "w1": (n((K, H)) / np.sqrt(K) / s).astype(np.float32),
        "gs": (np.random.uniform(0.5, 1.5, (K, 1)) / s).astype(np.float32),
        "gk": (np.random.uniform(0.5, 1.5, (K, 1)) * s).astype(np.float32),
        "d_words": packed_dT[0],
        "d_scales": packed_dT[1],
        "offs": striped(np.random.permutation(T)[:S]),
        "n1": striped(np.random.randint(0, S, W)),
        "n2": striped8(np.stack([np.random.permutation(S) for _ in range(8)])),
        "n3": striped8(np.stack([np.random.permutation(S) for _ in range(8)])),
        "cand": striped(np.random.permutation(T)[:C]),
        "k1": striped8(np.random.randint(0, G, (8, H))),
        "n4": striped(np.random.permutation(S)),
        "n5": striped(np.random.permutation(S)),
    }


def reference(x_words, x_scales, w1, gs, gk, d_words, d_scales, offs, n1, n2, n3, cand, k1, n4, n5):
    x_cand = unpack_weight(x_words, x_scales)[:, unstriped(cand)]
    xq = unpack_weight(x_words, x_scales)[:, unstriped(offs)]
    y = mxq(f64(w1), 0, "e4m3").T @ xq
    ex = np.exp(y)
    mb = ex[:, unstriped(n1)]
    ms = mb.reshape(H, S, 4).sum(axis=2)
    z = f64(gs) * (np.log(ms + ex) - y)
    a = 0.0625 * ((x_cand.T @ mxq(z, 0, "e4m3")))
    d_k1 = unpack_weight(d_words, d_scales)[np.arange(K)[:, None], runs(k1, K)]
    z2 = f64(gk) * (y * (sigmoid(y[np.arange(H)[:, None], runs(n2, H)] - (y[np.arange(H)[:, None], runs(n3, H)]))))
    b = 0.0625 * ((d_k1.T @ mxq(z2, 0, "e4m3")))
    return (a + a[:, unstriped(n4)]) * (sigmoid(b + b[:, unstriped(n5)]))

@@ -1,0 +1,251 @@
+from contextlib import ExitStack
+
+import concourse.mybir as mybir
+
+K, T, S, H, W, C, G = 512, 1024, 512, 512, 2048, 512, 2048
+FLOPS = 3 * 2 * 512 * 512 * 512
+
+F32 = mybir.dt.float32
+BF16 = mybir.dt.bfloat16
+I32 = mybir.dt.int32
+U32 = mybir.dt.uint32
+U16 = mybir.dt.uint16
+U8 = mybir.dt.uint8
+FP8X4 = mybir.dt.float8_e4m3fn_x4
+ACT = mybir.ActivationFunctionType
+ALU = mybir.AluOpType
+
+P = 128
+PACK = 4
+MEMBERS = 4
+SPARE = 16
+CHUNKS = 4
+CW = S // CHUNKS
+
+
+def tile_picked_cdkeytriebglsecmp_none_p_kernel(
+    tc, x_words, x_scales, w1, gs, gk, d_words, d_scales, offs, n1, n2, n3, cand, k1, n4, n5, out
+):
+    nc = tc.nc
+    with ExitStack() as ctx:
+        lists = ctx.enter_context(tc.tile_pool(name="lists", bufs=1))
+        keep = ctx.enter_context(tc.tile_pool(name="keep", bufs=1))
+        ring = ctx.enter_context(tc.tile_pool(name="ring", bufs=2))
+        psum = ctx.enter_context(tc.psum_pool(name="psum", bufs=1))
+
+        def load_list(name, src):
+            tile = lists.tile(list(src.shape), U16, name=name)
+            nc.sync.dma_start(tile[:], src)
+            return tile
+
+        def entries(tile, first, count):
+            return tile[:, first // 16 : (first + count) // 16]
+
+        def fetch(dst, window, offsets):
+            nc.scalar.activation(dst, window[:].indirect(offsets), ACT.Copy)
+
+        def window_tile(name, width):
+            tile = keep.tile([P, width], F32, name=name, tag=name)
+            nc.vector.memset(tile[:, S:width], 0.0)
+            return tile
+
+        def interleave(dst, src):
+            nc.vector.tensor_copy(
+                out=dst.rearrange("p (c i) t -> p c t i", i=4),
+                in_=src.rearrange("p t (c i) -> p c t i", i=4),
+            )
+
+        def mx(acc, lhs_w, lhs_s, rhs_w, rhs_s):
+            nc.tensor.matmul_mx(
+                out=acc,
+                lhsT=lhs_w.bitcast(FP8X4),
+                lhsT_scale=lhs_s,
+                rhs=rhs_w.bitcast(FP8X4),
+                rhs_scale=rhs_s,
+                start=True,
+                stop=True,
+            )
+
+        xs_tab = keep.tile([P, T], U8, name="xs_tab", align_bytes=64)
+        nc.vector.memset(xs_tab[:].bitcast(I32), 0)
+        offs_t = load_list("offs_t", offs)
+        for q in range(4):
+            nc.scalar.dma_start(
+                xs_tab[32 * q : 32 * q + 4, :].bitcast(I32), x_scales[0][4 * q : 4 * q + 4, :].bitcast(I32)
+            )
+        xw_tab = keep.tile([P, T], U32, name="xw_tab", align_bytes=64)
+        nc.sync.dma_start(xw_tab[:].bitcast(I32), x_words[0].rearrange("p n t -> p (n t)").bitcast(I32))
+        w_rows = w1.rearrange("(p j) c -> p j c", j=PACK)
+        w_raw = []
+        for h in range(2):
+            tile = keep.tile([P, PACK, H // 2], F32, name="w_raw%d" % h)
+            nc.sync.dma_start(tile[:], w_rows[:, :, h * H // 2 : (h + 1) * H // 2])
+            w_raw.append(tile)
+        n2_t = load_list("n2_t", n2)
+        n3_t = load_list("n3_t", n3)
+        n1_t = load_list("n1_t", n1)
+        gk_t = keep.tile([P, PACK], F32, name="gk_t")
+        nc.sync.dma_start(gk_t[:], gk.rearrange("(p t) o -> p (t o)", t=PACK))
+        gs_t = keep.tile([P, PACK], F32, name="gs_t")
+        nc.sync.dma_start(gs_t[:], gs.rearrange("(p t) o -> p (t o)", t=PACK))
+        k1_t = load_list("k1_t", k1)
+        ds_tab = keep.tile([P, G], U8, name="ds_tab", align_bytes=64)
+        nc.vector.memset(ds_tab[:].bitcast(I32), 0)
+        for e in range(2):
+            nc.sync.dma_start(ds_tab[e:P:16, :].bitcast(I32), d_scales[0][e:16:2, :].bitcast(I32))
+        dw_tab = keep.tile([P, G], U32, name="dw_tab", align_bytes=64)
+        nc.sync.dma_start(dw_tab[:].bitcast(I32), d_words[0].rearrange("p n t -> p (n t)").bitcast(I32))
+        cand_t = load_list("cand_t", cand)
+        n5_t = load_list("n5_t", n5)
+        n4_t = load_list("n4_t", n4)
+
+        y_sb = [window_tile("y_sb%d" % t, 2 * S) for t in range(PACK)]
+        ex = [window_tile("ex%d" % t, S + SPARE) for t in range(PACK)]
+        b_sb = [window_tile("b_sb%d" % u, S + SPARE) for u in range(4)]
+        a_sb = [window_tile("a_sb%d" % u, S + SPARE) for u in range(4)]
+        dk_s = keep.tile([P, H], U8, name="dk_s", align_bytes=64)
+        nc.vector.memset(dk_s[:].bitcast(I32), 0)
+
+        xq_w = keep.tile([P, S], U32, name="xq_w", align_bytes=64)
+        xq_s = keep.tile([P, S], U8, name="xq_s", align_bytes=64)
+        nc.vector.tensor_copy(xq_w[:], xw_tab[:].indirect(offs_t[:]))
+        nc.vector.tensor_copy(xq_s[:], xs_tab[:].indirect(offs_t[:]))
+
+        w_bf = keep.tile([P, PACK, P, PACK], BF16, name="w_bf", align_bytes=64)
+        halves = [
+            (
+                w_bf[:, :, h * P // 2 : (h + 1) * P // 2, :].rearrange("p t m j -> p m j t"),
+                w_raw[h][:].rearrange("p j (m t) -> p m j t", t=PACK),
+            )
+            for h in range(2)
+        ]
+        nc.scalar.activation(halves[0][0], halves[0][1], ACT.Copy)
+        nc.vector.tensor_copy(halves[1][0], halves[1][1])
+        wq_w = keep.tile([P, PACK, P], U32, name="wq_w", align_bytes=64)
+        wq_s = keep.tile([P, PACK, P], U8, name="wq_s", align_bytes=64)
+        y_ps = []
+        for t in range(PACK):
+            nc.vector.quantize_mx(
+                out=wq_w[:, t, :].bitcast(FP8X4),
+                scales=wq_s[:, t, :],
+                in_=w_bf[:, t].rearrange("p m j -> p (m j)"),
+            )
+            bank = psum.tile([P, S], F32, name="y_ps%d" % t, tag="ya%d" % t)
+            mx(bank[:], wq_w[:, t, :], wq_s[:, t, :], xq_w[:], xq_s[:])
+            nc.scalar.activation(ex[t][:, :S], bank[:], ACT.Exp)
+            y_ps.append(bank)
+
+        diff = keep.tile([P, PACK, S], F32, name="diff", tag="diff_log")
+        z2_pl = keep.tile([P, PACK, S], BF16, name="z2_pl")
+        for t in range(PACK):
+            nc.vector.tensor_copy(y_sb[t][:, :S], y_ps[t][:])
+        for t in range(PACK):
+            g2 = ring.tile([P, S], F32, name="g2")
+            g3 = ring.tile([P, S], F32, name="g3")
+            fetch(g2[:], y_sb[t], n2_t[:])
+            fetch(g3[:], y_sb[t], n3_t[:])
+            nc.vector.tensor_tensor(diff[:, t, :], g2[:], g3[:], ALU.subtract)
+            th = ring.tile([P, S], F32, name="th")
+            nc.scalar.activation(th[:], diff[:, t, :], ACT.Tanh, scale=0.5)
+            ygk = ring.tile([P, S], F32, name="ygk")
+            nc.vector.tensor_scalar(ygk[:], y_sb[t][:, :S], gk_t[:, t : t + 1], 0.5, ALU.mult, ALU.mult)
+            nc.vector.scalar_tensor_tensor(z2_pl[:, t, :], th[:], 1.0, ygk[:], ALU.add, ALU.mult)
+
+        dk_w = keep.tile([P, H], U32, name="dk_w", align_bytes=64)
+        dk_raw = keep.tile([P, H], U8, name="dk_raw", align_bytes=64)
+        nc.vector.tensor_copy(dk_raw[:], ds_tab[:].indirect(k1_t[:]))
+        for src, dst in ((0, 0), (1, 1), (16, 2), (17, 3)):
+            nc.sync.dma_start(dk_s[dst:P:32, :].bitcast(I32), dk_raw[src:P:32, :].bitcast(I32))
+        nc.vector.tensor_copy(dk_w[:], dw_tab[:].indirect(k1_t[:]))
+
+        z2_w = keep.tile([P, S], U32, name="z2_w", align_bytes=64)
+        z2_s = keep.tile([P, S], U8, name="z2_s", align_bytes=64)
+        for h in range(2):
+            cols = slice(h * S // 2, (h + 1) * S // 2)
+            z2_bf = ring.tile([P, S // 2, PACK], BF16, name="z2_bf", align_bytes=64)
+            interleave(z2_bf[:], z2_pl[:, :, cols])
+            nc.vector.quantize_mx(
+                out=z2_w[:, cols].bitcast(FP8X4), scales=z2_s[:, cols], in_=z2_bf[:].rearrange("p j t -> p (j t)")
+            )
+        b_ps = []
+        for u in range(4):
+            rows = slice(u * P, (u + 1) * P)
+            bank = psum.tile([P, S], F32, name="b_ps%d" % u)
+            mx(bank[:], dk_w[:, rows], dk_s[:, rows], z2_w[:], z2_s[:])
+            b_ps.append(bank)
+
+        ygs = keep.tile([P, PACK, S], F32, name="ygs")
+        xc_w = keep.tile([P, C], U32, name="xc_w", align_bytes=64)
+        xc_s = keep.tile([P, C], U8, name="xc_s", align_bytes=64)
+        total = keep.tile([P, CHUNKS, PACK, CW], F32, name="total", tag="total_gate")
+        logs = keep.tile([P, CHUNKS, PACK, CW], F32, name="logs", tag="diff_log")
+        z_w = keep.tile([P, S], U32, name="z_w", align_bytes=64)
+        z_s = keep.tile([P, S], U8, name="z_s", align_bytes=64)
+        a_ps = [psum.tile([P, S], F32, name="a_ps%d" % u, tag="ya%d" % u) for u in range(4)]
+
+        def members(c):
+            cols = slice(c * CW, (c + 1) * CW)
+            for t in range(PACK):
+                mb = ring.tile([P, CW, MEMBERS], F32, name="mb", bufs=6)
+                fetch(mb[:].rearrange("p j m -> p (j m)"), ex[t], entries(n1_t, c * CW * MEMBERS, CW * MEMBERS))
+                ms = ring.tile([P, CW], F32, name="ms", bufs=4)
+                nc.vector.tensor_reduce(ms[:], mb[:], mybir.AxisListType.X, ALU.add)
+                nc.vector.tensor_tensor(total[:, c, t, :], ms[:], ex[t][:, cols], ALU.add)
+
+        def finish_z(c):
+            cols = slice(c * CW, (c + 1) * CW)
+            nc.scalar.activation(logs[:, c], total[:, c], ACT.Ln)
+            z_pl = ring.tile([P, PACK, CW], BF16, name="z_pl")
+            for t in range(PACK):
+                nc.vector.scalar_tensor_tensor(
+                    z_pl[:, t, :], logs[:, c, t, :], gs_t[:, t : t + 1], ygs[:, t, cols], ALU.mult, ALU.subtract
+                )
+            z_bf = ring.tile([P, CW, PACK], BF16, name="z_bf", align_bytes=64)
+            interleave(z_bf[:], z_pl[:])
+            nc.vector.quantize_mx(
+                out=z_w[:, cols].bitcast(FP8X4), scales=z_s[:, cols], in_=z_bf[:].rearrange("p j t -> p (j t)")
+            )
+            for u in range(4):
+                rows = slice(u * P, (u + 1) * P)
+                mx(a_ps[u][:, cols], xc_w[:, rows], xc_s[:, rows], z_w[:, cols], z_s[:, cols])
+
+        b_sum = keep.tile([P, 4, S], F32, name="b_sum")
+
+        def b_pair(u):
+            b5 = ring.tile([P, S], F32, name="b5")
+            fetch(b5[:], b_sb[u], n5_t[:])
+            nc.vector.tensor_tensor(b_sum[:, u, :], b5[:], b_sb[u][:, :S], ALU.add)
+
+        members(0)
+        for t in range(PACK):
+            nc.vector.tensor_scalar(ygs[:, t, :], y_sb[t][:, :S], gs_t[:, t : t + 1], None, ALU.mult)
+        nc.vector.tensor_copy(xc_w[:], xw_tab[:].indirect(cand_t[:]))
+        nc.vector.tensor_copy(xc_s[:], xs_tab[:].indirect(cand_t[:]))
+        for c in range(1, CHUNKS):
+            members(c)
+            finish_z(c - 1)
+        for u in range(4):
+            nc.vector.tensor_copy(b_sb[u][:, :S], b_ps[u][:])
+        b_pair(0)
+        finish_z(CHUNKS - 1)
+        for u in range(1, 4):
+            b_pair(u)
+
+        for u in range(4):
+            nc.vector.tensor_copy(a_sb[u][:, :S], a_ps[u][:])
+        for u in range(4):
+            gate = keep.tile(
+                [P, CHUNKS * S if u == 0 else S + SPARE], F32, name="gate%d" % u, tag="total_gate" if u == 0 else "a_sb%d" % u
+            )
+            a4 = ring.tile([P, S], F32, name="a4", bufs=4)
+            fetch(a4[:], a_sb[u], n4_t[:])
+            a_sum = ring.tile([P, S], F32, name="a_sum")
+            nc.vector.tensor_tensor(a_sum[:], a4[:], a_ps[u][:], ALU.add)
+            for first, count in [(0, S)] if u < 3 else [(0, S // 2), (S // 2, S // 2)]:
+                cols = slice(first, first + count)
+                nc.scalar.activation(gate[:, cols], b_sum[:, u, cols], ACT.Sigmoid, scale=0.0625)
+                res = ring.tile([P, S], F32, name="res", bufs=3)
+                nc.vector.scalar_tensor_tensor(
+                    res[:, :count], a_sum[:, cols], 0.0625, gate[:, cols], ALU.mult, ALU.mult
+                )
+                nc.sync.dma_start(out[u * P : (u + 1) * P, cols], res[:, :count])

@@ -1,6 +1,7 @@
 from contextlib import ExitStack
 
 import concourse.mybir as mybir
+from concourse.masks import make_identity
 
 K, T, S, H, W, C, G = 512, 1024, 512, 512, 2048, 512, 2048
 FLOPS = 3 * 2 * 512 * 512 * 512
@@ -67,11 +68,11 @@ def tile_picked_cdkeytriebglsecmp_none_p_kernel(
             )
 
         xs_tab = keep.tile([P, T], U8, name="xs_tab", align_bytes=64)
-        nc.vector.memset(xs_tab[:].bitcast(I32), 0)
         offs_t = load_list("offs_t", offs)
         for q in range(4):
-            nc.scalar.dma_start(
-                xs_tab[32 * q : 32 * q + 4, :].bitcast(I32), x_scales[0][4 * q : 4 * q + 4, :].bitcast(I32)
+            nc.sync.dma_start(
+                xs_tab[32 * q : 32 * q + 32, :].bitcast(I32),
+                x_scales[0][4 * q : 4 * q + 4, :].bitcast(I32).partition_broadcast(8),
             )
         xw_tab = keep.tile([P, T], U32, name="xw_tab", align_bytes=64)
         nc.sync.dma_start(xw_tab[:].bitcast(I32), x_words[0].rearrange("p n t -> p (n t)").bitcast(I32))
@@ -106,25 +107,33 @@ def tile_picked_cdkeytriebglsecmp_none_p_kernel(
         dk_s = keep.tile([P, H], U8, name="dk_s", align_bytes=64)
         nc.vector.memset(dk_s[:].bitcast(I32), 0)
 
-        xq_w = keep.tile([P, S], U32, name="xq_w", align_bytes=64)
-        xq_s = keep.tile([P, S], U8, name="xq_s", align_bytes=64)
-        nc.vector.tensor_copy(xq_w[:], xw_tab[:].indirect(offs_t[:]))
+        xq_w = keep.tile([P, S], U32, name="xq_w", tag="x_picked_w", align_bytes=64)
+        xq_s = keep.tile([P, S], U8, name="xq_s", tag="x_picked_s", align_bytes=64)
         nc.vector.tensor_copy(xq_s[:], xs_tab[:].indirect(offs_t[:]))
+        nc.vector.tensor_copy(xq_w[:], xw_tab[:].indirect(offs_t[:]))
+        ident = keep.tile([P, P], F32, name="ident")
+        make_identity(nc, ident[:])
 
         w_bf = keep.tile([P, PACK, P, PACK], BF16, name="w_bf", align_bytes=64)
-        halves = [
-            (
-                w_bf[:, :, h * P // 2 : (h + 1) * P // 2, :].rearrange("p t m j -> p m j t"),
-                w_raw[h][:].rearrange("p j (m t) -> p m j t", t=PACK),
-            )
-            for h in range(2)
-        ]
-        nc.scalar.activation(halves[0][0], halves[0][1], ACT.Copy)
-        nc.vector.tensor_copy(halves[1][0], halves[1][1])
-        wq_w = keep.tile([P, PACK, P], U32, name="wq_w", align_bytes=64)
-        wq_s = keep.tile([P, PACK, P], U8, name="wq_s", align_bytes=64)
+
+        def w_views(h, t):
+            dst = w_bf[:, t, h * P // 2 : (h + 1) * P // 2, :]
+            src = w_raw[h][:].rearrange("p j (m t) -> p t m j", t=PACK)[:, t]
+            return dst, src
+
+        for h, t in ((0, 0), (0, 1), (1, 1)):
+            dst, src = w_views(h, t)
+            nc.scalar.activation(dst, src, ACT.Copy)
+        for t in (2, 3):
+            dst, src = w_views(0, t)
+            nc.vector.tensor_copy(dst, src)
+        wq_w = keep.tile([P, PACK, P], U32, name="wq_w", tag="left_w", align_bytes=64)
+        wq_s = keep.tile([P, PACK, P], U8, name="wq_s", tag="left_s", align_bytes=64)
         y_ps = []
         for t in range(PACK):
+            if t != 1:
+                dst, src = w_views(1, t)
+                nc.vector.tensor_copy(dst, src)
             nc.vector.quantize_mx(
                 out=wq_w[:, t, :].bitcast(FP8X4),
                 scales=wq_s[:, t, :],
@@ -151,8 +160,8 @@ def tile_picked_cdkeytriebglsecmp_none_p_kernel(
             nc.vector.tensor_scalar(ygk[:], y_sb[t][:, :S], gk_t[:, t : t + 1], 0.5, ALU.mult, ALU.mult)
             nc.vector.scalar_tensor_tensor(z2_pl[:, t, :], th[:], 1.0, ygk[:], ALU.add, ALU.mult)
 
-        dk_w = keep.tile([P, H], U32, name="dk_w", align_bytes=64)
-        dk_raw = keep.tile([P, H], U8, name="dk_raw", align_bytes=64)
+        dk_w = keep.tile([P, H], U32, name="dk_w", tag="left_w", align_bytes=64)
+        dk_raw = keep.tile([P, H], U8, name="dk_raw", tag="left_s", align_bytes=64)
         nc.vector.tensor_copy(dk_raw[:], ds_tab[:].indirect(k1_t[:]))
         for src, dst in ((0, 0), (1, 1), (16, 2), (17, 3)):
             nc.sync.dma_start(dk_s[dst:P:32, :].bitcast(I32), dk_raw[src:P:32, :].bitcast(I32))
@@ -170,49 +179,63 @@ def tile_picked_cdkeytriebglsecmp_none_p_kernel(
         b_ps = []
         for u in range(4):
             rows = slice(u * P, (u + 1) * P)
-            bank = psum.tile([P, S], F32, name="b_ps%d" % u)
+            bank = psum.tile([P, S], F32, name="b_ps%d" % u, tag="ba%d" % u)
             mx(bank[:], dk_w[:, rows], dk_s[:, rows], z2_w[:], z2_s[:])
             b_ps.append(bank)
 
         ygs = keep.tile([P, PACK, S], F32, name="ygs")
-        xc_w = keep.tile([P, C], U32, name="xc_w", align_bytes=64)
-        xc_s = keep.tile([P, C], U8, name="xc_s", align_bytes=64)
-        total = keep.tile([P, CHUNKS, PACK, CW], F32, name="total", tag="total_gate")
+        xc_w = keep.tile([P, C], U32, name="xc_w", tag="x_picked_w", align_bytes=64)
+        xc_s = keep.tile([P, C], U8, name="xc_s", tag="x_picked_s", align_bytes=64)
         logs = keep.tile([P, CHUNKS, PACK, CW], F32, name="logs", tag="diff_log")
         z_w = keep.tile([P, S], U32, name="z_w", align_bytes=64)
         z_s = keep.tile([P, S], U8, name="z_s", align_bytes=64)
-        a_ps = [psum.tile([P, S], F32, name="a_ps%d" % u, tag="ya%d" % u) for u in range(4)]
+        a_ps = [psum.tile([P, S], F32, name="a_ps%d" % u, tag="ba%d" % u) for u in range(4)]
+
+        def turn(dst, src, start, stop):
+            nc.tensor.matmul(dst, src, ident[:], start=start, stop=stop, is_transpose=True)
+
+        totals = {}
 
         def members(c):
             cols = slice(c * CW, (c + 1) * CW)
+            totals[c] = psum.tile([P, PACK, P], F32, name="total%d" % c, tag="ya%d" % (c % 2))
             for t in range(PACK):
                 mb = ring.tile([P, CW, MEMBERS], F32, name="mb", bufs=6)
                 fetch(mb[:].rearrange("p j m -> p (j m)"), ex[t], entries(n1_t, c * CW * MEMBERS, CW * MEMBERS))
-                ms = ring.tile([P, CW], F32, name="ms", bufs=4)
-                nc.vector.tensor_reduce(ms[:], mb[:], mybir.AxisListType.X, ALU.add)
-                nc.vector.tensor_tensor(total[:, c, t, :], ms[:], ex[t][:, cols], ALU.add)
+                pair = ring.tile([P, CW, 2], F32, name="pair", bufs=4)
+                nc.vector.tensor_tensor(pair[:], mb[:, :, 0:2], mb[:, :, 2:4], ALU.add)
+                turn(totals[c][:, t, :], ex[t][:, cols], True, False)
+                turn(totals[c][:, t, :], pair[:, :, 0], False, False)
+                turn(totals[c][:, t, :], pair[:, :, 1], False, True)
 
         def finish_z(c):
             cols = slice(c * CW, (c + 1) * CW)
-            nc.scalar.activation(logs[:, c], total[:, c], ACT.Ln)
+            nc.scalar.activation(logs[:, c], totals[c][:], ACT.Ln)
+            back = psum.tile([P, PACK, CW], F32, name="back%d" % c, tag="ya%d" % (2 + c % 2))
+            for t in range(PACK):
+                turn(back[:, t, :], logs[:, c, t, :], True, True)
             z_pl = ring.tile([P, PACK, CW], BF16, name="z_pl")
             for t in range(PACK):
                 nc.vector.scalar_tensor_tensor(
-                    z_pl[:, t, :], logs[:, c, t, :], gs_t[:, t : t + 1], ygs[:, t, cols], ALU.mult, ALU.subtract
+                    z_pl[:, t, :], back[:, t, :], gs_t[:, t : t + 1], ygs[:, t, cols], ALU.mult, ALU.subtract
                 )
             z_bf = ring.tile([P, CW, PACK], BF16, name="z_bf", align_bytes=64)
             interleave(z_bf[:], z_pl[:])
             nc.vector.quantize_mx(
                 out=z_w[:, cols].bitcast(FP8X4), scales=z_s[:, cols], in_=z_bf[:].rearrange("p j t -> p (j t)")
             )
-            for u in range(4):
-                rows = slice(u * P, (u + 1) * P)
-                mx(a_ps[u][:, cols], xc_w[:, rows], xc_s[:, rows], z_w[:, cols], z_s[:, cols])
+            if c % 2 == 1:
+                half = slice((c - 1) * CW, (c + 1) * CW)
+                for u in range(4):
+                    rows = slice(u * P, (u + 1) * P)
+                    mx(a_ps[u][:, half], xc_w[:, rows], xc_s[:, rows], z_w[:, half], z_s[:, half])
+                for u in range(4):
+                    nc.vector.tensor_copy(a_sb[u][:, half], a_ps[u][:, half])
 
         b_sum = keep.tile([P, 4, S], F32, name="b_sum")
 
         def b_pair(u):
-            b5 = ring.tile([P, S], F32, name="b5")
+            b5 = keep.tile([P, S], F32, name="b5_%d" % u, tag="ex%d" % u)
             fetch(b5[:], b_sb[u], n5_t[:])
             nc.vector.tensor_tensor(b_sum[:, u, :], b5[:], b_sb[u][:, :S], ALU.add)
 
@@ -221,31 +244,28 @@ def tile_picked_cdkeytriebglsecmp_none_p_kernel(
             nc.vector.tensor_scalar(ygs[:, t, :], y_sb[t][:, :S], gs_t[:, t : t + 1], None, ALU.mult)
         nc.vector.tensor_copy(xc_w[:], xw_tab[:].indirect(cand_t[:]))
         nc.vector.tensor_copy(xc_s[:], xs_tab[:].indirect(cand_t[:]))
+        for u in range(4):
+            nc.vector.tensor_copy(b_sb[u][:, :S], b_ps[u][:])
         for c in range(1, CHUNKS):
             members(c)
             finish_z(c - 1)
-        for u in range(4):
-            nc.vector.tensor_copy(b_sb[u][:, :S], b_ps[u][:])
         b_pair(0)
         finish_z(CHUNKS - 1)
         for u in range(1, 4):
             b_pair(u)
 
         for u in range(4):
-            nc.vector.tensor_copy(a_sb[u][:, :S], a_ps[u][:])
-        for u in range(4):
             gate = keep.tile(
-                [P, CHUNKS * S if u == 0 else S + SPARE], F32, name="gate%d" % u, tag="total_gate" if u == 0 else "a_sb%d" % u
+                [P, CHUNKS * S if u == 0 else S + SPARE], F32, name="gate%d" % u, tag="diff_log" if u == 0 else "a_sb%d" % u
             )
+            pieces = [slice(0, S)] if u < 3 else [slice(0, S // 2), slice(S // 2, S)]
             a4 = ring.tile([P, S], F32, name="a4", bufs=4)
-            fetch(a4[:], a_sb[u], n4_t[:])
-            a_sum = ring.tile([P, S], F32, name="a_sum")
-            nc.vector.tensor_tensor(a_sum[:], a4[:], a_ps[u][:], ALU.add)
-            for first, count in [(0, S)] if u < 3 else [(0, S // 2), (S // 2, S // 2)]:
-                cols = slice(first, first + count)
+            a_sum = ring.tile([P, S], F32, name="a_sum", bufs=4)
+            for cols in pieces:
+                fetch(a4[:, cols], a_sb[u], entries(n4_t, cols.start, cols.stop - cols.start))
+                nc.vector.tensor_tensor(a_sum[:, cols], a4[:, cols], a_ps[u][:, cols], ALU.add)
+            for cols in pieces:
                 nc.scalar.activation(gate[:, cols], b_sum[:, u, cols], ACT.Sigmoid, scale=0.0625)
-                res = ring.tile([P, S], F32, name="res", bufs=3)
-                nc.vector.scalar_tensor_tensor(
-                    res[:, :count], a_sum[:, cols], 0.0625, gate[:, cols], ALU.mult, ALU.mult
-                )
-                nc.sync.dma_start(out[u * P : (u + 1) * P, cols], res[:, :count])
+                res = ring.tile([P, S], F32, name="res", bufs=5)
+                nc.vector.scalar_tensor_tensor(res[:, cols], a_sum[:, cols], 0.0625, gate[:, cols], ALU.mult, ALU.mult)
+                nc.sync.dma_start(out[u * P : (u + 1) * P, cols], res[:, cols])

@@ -68,20 +68,18 @@ def tile_picked_cdkeytriebglsecmp_none_p_kernel(
             )
 
         xs_tab = keep.tile([P, T], U8, name="xs_tab", align_bytes=64)
+        w_rows = w1.rearrange("(p j) c -> p j c", j=PACK)
+        w_raw = [keep.tile([P, PACK, H // 2], F32, name="w_raw%d" % h) for h in range(2)]
+        xw_tab = keep.tile([P, T], U32, name="xw_tab", align_bytes=64)
+        nc.sync.dma_start(xw_tab[:].bitcast(I32), x_words[0].rearrange("p n t -> p (n t)").bitcast(I32))
         offs_t = load_list("offs_t", offs)
         for q in range(4):
             nc.sync.dma_start(
                 xs_tab[32 * q : 32 * q + 32, :].bitcast(I32),
                 x_scales[0][4 * q : 4 * q + 4, :].bitcast(I32).partition_broadcast(8),
             )
-        xw_tab = keep.tile([P, T], U32, name="xw_tab", align_bytes=64)
-        nc.sync.dma_start(xw_tab[:].bitcast(I32), x_words[0].rearrange("p n t -> p (n t)").bitcast(I32))
-        w_rows = w1.rearrange("(p j) c -> p j c", j=PACK)
-        w_raw = []
         for h in range(2):
-            tile = keep.tile([P, PACK, H // 2], F32, name="w_raw%d" % h)
-            nc.sync.dma_start(tile[:], w_rows[:, :, h * H // 2 : (h + 1) * H // 2])
-            w_raw.append(tile)
+            nc.sync.dma_start(w_raw[h][:], w_rows[:, :, h * H // 2 : (h + 1) * H // 2])
         n2_t = load_list("n2_t", n2)
         n3_t = load_list("n3_t", n3)
         n1_t = load_list("n1_t", n1)
@@ -109,8 +107,8 @@ def tile_picked_cdkeytriebglsecmp_none_p_kernel(
 
         xq_w = keep.tile([P, S], U32, name="xq_w", tag="x_picked_w", align_bytes=64)
         xq_s = keep.tile([P, S], U8, name="xq_s", tag="x_picked_s", align_bytes=64)
-        nc.vector.tensor_copy(xq_s[:], xs_tab[:].indirect(offs_t[:]))
         nc.vector.tensor_copy(xq_w[:], xw_tab[:].indirect(offs_t[:]))
+        nc.vector.tensor_copy(xq_s[:], xs_tab[:].indirect(offs_t[:]))
         ident = keep.tile([P, P], F32, name="ident")
         make_identity(nc, ident[:])
 
@@ -121,19 +119,15 @@ def tile_picked_cdkeytriebglsecmp_none_p_kernel(
             src = w_raw[h][:].rearrange("p j (m t) -> p t m j", t=PACK)[:, t]
             return dst, src
 
-        for h, t in ((0, 0), (0, 1), (1, 1)):
-            dst, src = w_views(h, t)
-            nc.scalar.activation(dst, src, ACT.Copy)
-        for t in (2, 3):
+        for t in range(PACK):
             dst, src = w_views(0, t)
-            nc.vector.tensor_copy(dst, src)
+            nc.scalar.activation(dst, src, ACT.Copy)
         wq_w = keep.tile([P, PACK, P], U32, name="wq_w", tag="left_w", align_bytes=64)
         wq_s = keep.tile([P, PACK, P], U8, name="wq_s", tag="left_s", align_bytes=64)
         y_ps = []
         for t in range(PACK):
-            if t != 1:
-                dst, src = w_views(1, t)
-                nc.vector.tensor_copy(dst, src)
+            dst, src = w_views(1, t)
+            nc.vector.tensor_copy(dst, src)
             nc.vector.quantize_mx(
                 out=wq_w[:, t, :].bitcast(FP8X4),
                 scales=wq_s[:, t, :],
@@ -202,7 +196,10 @@ def tile_picked_cdkeytriebglsecmp_none_p_kernel(
             for t in range(PACK):
                 mb = ring.tile([P, CW, MEMBERS], F32, name="mb", bufs=6)
                 fetch(mb[:].rearrange("p j m -> p (j m)"), ex[t], entries(n1_t, c * CW * MEMBERS, CW * MEMBERS))
-                pair = ring.tile([P, CW, 2], F32, name="pair", bufs=4)
+                if (c, t) == (CHUNKS - 1, PACK - 1):
+                    pair = keep.tile([P, CW, 2], F32, name="last_pair", tag="pair_b5")
+                else:
+                    pair = ring.tile([P, CW, 2], F32, name="pair", bufs=4)
                 nc.vector.tensor_tensor(pair[:], mb[:, :, 0:2], mb[:, :, 2:4], ALU.add)
                 turn(totals[c][:, t, :], ex[t][:, cols], True, False)
                 turn(totals[c][:, t, :], pair[:, :, 0], False, False)
@@ -224,8 +221,8 @@ def tile_picked_cdkeytriebglsecmp_none_p_kernel(
             nc.vector.quantize_mx(
                 out=z_w[:, cols].bitcast(FP8X4), scales=z_s[:, cols], in_=z_bf[:].rearrange("p j t -> p (j t)")
             )
-            if c % 2 == 1:
-                half = slice((c - 1) * CW, (c + 1) * CW)
+            if c > 0:
+                half = slice(0 if c == 1 else c * CW, (c + 1) * CW)
                 for u in range(4):
                     rows = slice(u * P, (u + 1) * P)
                     mx(a_ps[u][:, half], xc_w[:, rows], xc_s[:, rows], z_w[:, half], z_s[:, half])
@@ -234,10 +231,9 @@ def tile_picked_cdkeytriebglsecmp_none_p_kernel(
 
         b_sum = keep.tile([P, 4, S], F32, name="b_sum")
 
-        def b_pair(u):
-            b5 = keep.tile([P, S], F32, name="b5_%d" % u, tag="ex%d" % u)
-            fetch(b5[:], b_sb[u], n5_t[:])
-            nc.vector.tensor_tensor(b_sum[:, u, :], b5[:], b_sb[u][:, :S], ALU.add)
+        def b_pair(u, b5):
+            fetch(b5, b_sb[u], n5_t[:])
+            nc.vector.tensor_tensor(b_sum[:, u, :], b5, b_sb[u][:, :S], ALU.add)
 
         members(0)
         for t in range(PACK):
@@ -249,16 +245,18 @@ def tile_picked_cdkeytriebglsecmp_none_p_kernel(
         for c in range(1, CHUNKS):
             members(c)
             finish_z(c - 1)
-        b_pair(0)
+        b5_first = keep.tile([P, S], F32, name="b5_first", tag="ex0")
+        b_pair(0, b5_first[:])
         finish_z(CHUNKS - 1)
+        b5_rest = keep.tile([P, 3, S], F32, name="b5_rest", tag="pair_b5")
         for u in range(1, 4):
-            b_pair(u)
+            b_pair(u, b5_rest[:, u - 1, :])
 
         for u in range(4):
             gate = keep.tile(
                 [P, CHUNKS * S if u == 0 else S + SPARE], F32, name="gate%d" % u, tag="diff_log" if u == 0 else "a_sb%d" % u
             )
-            pieces = [slice(0, S)] if u < 3 else [slice(0, S // 2), slice(S // 2, S)]
+            pieces = [slice(0, S)] if u < 3 else [slice(0, S - P), slice(S - P, S)]
             a4 = ring.tile([P, S], F32, name="a4", bufs=4)
             a_sum = ring.tile([P, S], F32, name="a_sum", bufs=4)
             for cols in pieces:

from contextlib import ExitStack

import concourse.mybir as mybir
from concourse.masks import make_identity

K, T, S, H, W, C, G = 512, 1024, 512, 512, 2048, 512, 2048
FLOPS = 3 * 2 * 512 * 512 * 512

F32 = mybir.dt.float32
BF16 = mybir.dt.bfloat16
I32 = mybir.dt.int32
U32 = mybir.dt.uint32
U16 = mybir.dt.uint16
U8 = mybir.dt.uint8
FP8X4 = mybir.dt.float8_e4m3fn_x4
ACT = mybir.ActivationFunctionType
ALU = mybir.AluOpType

P = 128
PACK = 4
MEMBERS = 4
SPARE = 16
CHUNKS = 4
CW = S // CHUNKS


def tile_picked_cdkeytriebglsecmp_none_p_kernel(
    tc, x_words, x_scales, w1, gs, gk, d_words, d_scales, offs, n1, n2, n3, cand, k1, n4, n5, out
):
    nc = tc.nc
    with ExitStack() as ctx:
        lists = ctx.enter_context(tc.tile_pool(name="lists", bufs=1))
        keep = ctx.enter_context(tc.tile_pool(name="keep", bufs=1))
        ring = ctx.enter_context(tc.tile_pool(name="ring", bufs=2))
        psum = ctx.enter_context(tc.psum_pool(name="psum", bufs=1))

        def load_list(name, src):
            tile = lists.tile(list(src.shape), U16, name=name)
            nc.sync.dma_start(tile[:], src)
            return tile

        def entries(tile, first, count):
            return tile[:, first // 16 : (first + count) // 16]

        def fetch(dst, window, offsets):
            nc.scalar.activation(dst, window[:].indirect(offsets), ACT.Copy)

        def window_tile(name, width):
            tile = keep.tile([P, width], F32, name=name, tag=name)
            nc.vector.memset(tile[:, S:width], 0.0)
            return tile

        def interleave(dst, src):
            nc.vector.tensor_copy(
                out=dst.rearrange("p (c i) t -> p c t i", i=4),
                in_=src.rearrange("p t (c i) -> p c t i", i=4),
            )

        def mx(acc, lhs_w, lhs_s, rhs_w, rhs_s):
            nc.tensor.matmul_mx(
                out=acc,
                lhsT=lhs_w.bitcast(FP8X4),
                lhsT_scale=lhs_s,
                rhs=rhs_w.bitcast(FP8X4),
                rhs_scale=rhs_s,
                start=True,
                stop=True,
            )

        xs_tab = keep.tile([P, T], U8, name="xs_tab", align_bytes=64)
        w_rows = w1.rearrange("(p j) c -> p j c", j=PACK)
        w_raw = [keep.tile([P, PACK, H // 2], F32, name="w_raw%d" % h) for h in range(2)]
        xw_tab = keep.tile([P, T], U32, name="xw_tab", align_bytes=64)
        nc.sync.dma_start(xw_tab[:].bitcast(I32), x_words[0].rearrange("p n t -> p (n t)").bitcast(I32))
        offs_t = load_list("offs_t", offs)
        for q in range(4):
            nc.sync.dma_start(
                xs_tab[32 * q : 32 * q + 32, :].bitcast(I32),
                x_scales[0][4 * q : 4 * q + 4, :].bitcast(I32).partition_broadcast(8),
            )
        for h in range(2):
            nc.sync.dma_start(w_raw[h][:], w_rows[:, :, h * H // 2 : (h + 1) * H // 2])
        n2_t = load_list("n2_t", n2)
        n3_t = load_list("n3_t", n3)
        n1_t = load_list("n1_t", n1)
        gk_t = keep.tile([P, PACK], F32, name="gk_t")
        nc.sync.dma_start(gk_t[:], gk.rearrange("(p t) o -> p (t o)", t=PACK))
        gs_t = keep.tile([P, PACK], F32, name="gs_t")
        nc.sync.dma_start(gs_t[:], gs.rearrange("(p t) o -> p (t o)", t=PACK))
        k1_t = load_list("k1_t", k1)
        ds_tab = keep.tile([P, G], U8, name="ds_tab", align_bytes=64)
        nc.vector.memset(ds_tab[:].bitcast(I32), 0)
        for e in range(2):
            nc.sync.dma_start(ds_tab[e:P:16, :].bitcast(I32), d_scales[0][e:16:2, :].bitcast(I32))
        dw_tab = keep.tile([P, G], U32, name="dw_tab", align_bytes=64)
        nc.sync.dma_start(dw_tab[:].bitcast(I32), d_words[0].rearrange("p n t -> p (n t)").bitcast(I32))
        cand_t = load_list("cand_t", cand)
        n5_t = load_list("n5_t", n5)
        n4_t = load_list("n4_t", n4)

        y_sb = [window_tile("y_sb%d" % t, 2 * S) for t in range(PACK)]
        ex = [window_tile("ex%d" % t, S + SPARE) for t in range(PACK)]
        b_sb = [window_tile("b_sb%d" % u, S + SPARE) for u in range(4)]
        a_sb = [window_tile("a_sb%d" % u, S + SPARE) for u in range(4)]
        dk_s = keep.tile([P, H], U8, name="dk_s", align_bytes=64)
        nc.vector.memset(dk_s[:].bitcast(I32), 0)

        xq_w = keep.tile([P, S], U32, name="xq_w", tag="x_picked_w", align_bytes=64)
        xq_s = keep.tile([P, S], U8, name="xq_s", tag="x_picked_s", align_bytes=64)
        nc.vector.tensor_copy(xq_w[:], xw_tab[:].indirect(offs_t[:]))
        nc.vector.tensor_copy(xq_s[:], xs_tab[:].indirect(offs_t[:]))
        ident = keep.tile([P, P], F32, name="ident")
        make_identity(nc, ident[:])

        w_bf = keep.tile([P, PACK, P, PACK], BF16, name="w_bf", align_bytes=64)

        def w_views(h, t):
            dst = w_bf[:, t, h * P // 2 : (h + 1) * P // 2, :]
            src = w_raw[h][:].rearrange("p j (m t) -> p t m j", t=PACK)[:, t]
            return dst, src

        for t in range(PACK):
            dst, src = w_views(0, t)
            nc.scalar.activation(dst, src, ACT.Copy)
        wq_w = keep.tile([P, PACK, P], U32, name="wq_w", tag="left_w", align_bytes=64)
        wq_s = keep.tile([P, PACK, P], U8, name="wq_s", tag="left_s", align_bytes=64)
        y_ps = []
        for t in range(PACK):
            dst, src = w_views(1, t)
            nc.vector.tensor_copy(dst, src)
            nc.vector.quantize_mx(
                out=wq_w[:, t, :].bitcast(FP8X4),
                scales=wq_s[:, t, :],
                in_=w_bf[:, t].rearrange("p m j -> p (m j)"),
            )
            bank = psum.tile([P, S], F32, name="y_ps%d" % t, tag="ya%d" % t)
            mx(bank[:], wq_w[:, t, :], wq_s[:, t, :], xq_w[:], xq_s[:])
            nc.scalar.activation(ex[t][:, :S], bank[:], ACT.Exp)
            y_ps.append(bank)

        diff = keep.tile([P, PACK, S], F32, name="diff", tag="diff_log")
        z2_pl = keep.tile([P, PACK, S], BF16, name="z2_pl")
        for t in range(PACK):
            nc.vector.tensor_copy(y_sb[t][:, :S], y_ps[t][:])
        for t in range(PACK):
            g2 = ring.tile([P, S], F32, name="g2")
            g3 = ring.tile([P, S], F32, name="g3")
            fetch(g2[:], y_sb[t], n2_t[:])
            fetch(g3[:], y_sb[t], n3_t[:])
            nc.vector.tensor_tensor(diff[:, t, :], g2[:], g3[:], ALU.subtract)
            th = ring.tile([P, S], F32, name="th")
            nc.scalar.activation(th[:], diff[:, t, :], ACT.Tanh, scale=0.5)
            ygk = ring.tile([P, S], F32, name="ygk")
            nc.vector.tensor_scalar(ygk[:], y_sb[t][:, :S], gk_t[:, t : t + 1], 0.5, ALU.mult, ALU.mult)
            nc.vector.scalar_tensor_tensor(z2_pl[:, t, :], th[:], 1.0, ygk[:], ALU.add, ALU.mult)

        dk_w = keep.tile([P, H], U32, name="dk_w", tag="left_w", align_bytes=64)
        dk_raw = keep.tile([P, H], U8, name="dk_raw", tag="left_s", align_bytes=64)
        nc.vector.tensor_copy(dk_raw[:], ds_tab[:].indirect(k1_t[:]))
        for src, dst in ((0, 0), (1, 1), (16, 2), (17, 3)):
            nc.sync.dma_start(dk_s[dst:P:32, :].bitcast(I32), dk_raw[src:P:32, :].bitcast(I32))
        nc.vector.tensor_copy(dk_w[:], dw_tab[:].indirect(k1_t[:]))

        z2_w = keep.tile([P, S], U32, name="z2_w", align_bytes=64)
        z2_s = keep.tile([P, S], U8, name="z2_s", align_bytes=64)
        for h in range(2):
            cols = slice(h * S // 2, (h + 1) * S // 2)
            z2_bf = ring.tile([P, S // 2, PACK], BF16, name="z2_bf", align_bytes=64)
            interleave(z2_bf[:], z2_pl[:, :, cols])
            nc.vector.quantize_mx(
                out=z2_w[:, cols].bitcast(FP8X4), scales=z2_s[:, cols], in_=z2_bf[:].rearrange("p j t -> p (j t)")
            )
        b_ps = []
        for u in range(4):
            rows = slice(u * P, (u + 1) * P)
            bank = psum.tile([P, S], F32, name="b_ps%d" % u, tag="ba%d" % u)
            mx(bank[:], dk_w[:, rows], dk_s[:, rows], z2_w[:], z2_s[:])
            b_ps.append(bank)

        ygs = keep.tile([P, PACK, S], F32, name="ygs")
        xc_w = keep.tile([P, C], U32, name="xc_w", tag="x_picked_w", align_bytes=64)
        xc_s = keep.tile([P, C], U8, name="xc_s", tag="x_picked_s", align_bytes=64)
        logs = keep.tile([P, CHUNKS, PACK, CW], F32, name="logs", tag="diff_log")
        z_w = keep.tile([P, S], U32, name="z_w", align_bytes=64)
        z_s = keep.tile([P, S], U8, name="z_s", align_bytes=64)
        a_ps = [psum.tile([P, S], F32, name="a_ps%d" % u, tag="ba%d" % u) for u in range(4)]

        def turn(dst, src, start, stop):
            nc.tensor.matmul(dst, src, ident[:], start=start, stop=stop, is_transpose=True)

        totals = {}

        def members(c):
            cols = slice(c * CW, (c + 1) * CW)
            totals[c] = psum.tile([P, PACK, P], F32, name="total%d" % c, tag="ya%d" % (c % 2))
            for t in range(PACK):
                mb = ring.tile([P, CW, MEMBERS], F32, name="mb", bufs=6)
                fetch(mb[:].rearrange("p j m -> p (j m)"), ex[t], entries(n1_t, c * CW * MEMBERS, CW * MEMBERS))
                if (c, t) == (CHUNKS - 1, PACK - 1):
                    pair = keep.tile([P, CW, 2], F32, name="last_pair", tag="pair_b5")
                else:
                    pair = ring.tile([P, CW, 2], F32, name="pair", bufs=4)
                nc.vector.tensor_tensor(pair[:], mb[:, :, 0:2], mb[:, :, 2:4], ALU.add)
                turn(totals[c][:, t, :], ex[t][:, cols], True, False)
                turn(totals[c][:, t, :], pair[:, :, 0], False, False)
                turn(totals[c][:, t, :], pair[:, :, 1], False, True)

        def finish_z(c):
            cols = slice(c * CW, (c + 1) * CW)
            nc.scalar.activation(logs[:, c], totals[c][:], ACT.Ln)
            back = psum.tile([P, PACK, CW], F32, name="back%d" % c, tag="ya%d" % (2 + c % 2))
            for t in range(PACK):
                turn(back[:, t, :], logs[:, c, t, :], True, True)
            z_pl = ring.tile([P, PACK, CW], BF16, name="z_pl")
            for t in range(PACK):
                nc.vector.scalar_tensor_tensor(
                    z_pl[:, t, :], back[:, t, :], gs_t[:, t : t + 1], ygs[:, t, cols], ALU.mult, ALU.subtract
                )
            z_bf = ring.tile([P, CW, PACK], BF16, name="z_bf", align_bytes=64)
            interleave(z_bf[:], z_pl[:])
            nc.vector.quantize_mx(
                out=z_w[:, cols].bitcast(FP8X4), scales=z_s[:, cols], in_=z_bf[:].rearrange("p j t -> p (j t)")
            )
            if c > 0:
                half = slice(0 if c == 1 else c * CW, (c + 1) * CW)
                for u in range(4):
                    rows = slice(u * P, (u + 1) * P)
                    mx(a_ps[u][:, half], xc_w[:, rows], xc_s[:, rows], z_w[:, half], z_s[:, half])
                for u in range(4):
                    nc.vector.tensor_copy(a_sb[u][:, half], a_ps[u][:, half])

        b_sum = keep.tile([P, 4, S], F32, name="b_sum")

        def b_pair(u, b5):
            fetch(b5, b_sb[u], n5_t[:])
            nc.vector.tensor_tensor(b_sum[:, u, :], b5, b_sb[u][:, :S], ALU.add)

        members(0)
        for t in range(PACK):
            nc.vector.tensor_scalar(ygs[:, t, :], y_sb[t][:, :S], gs_t[:, t : t + 1], None, ALU.mult)
        nc.vector.tensor_copy(xc_w[:], xw_tab[:].indirect(cand_t[:]))
        nc.vector.tensor_copy(xc_s[:], xs_tab[:].indirect(cand_t[:]))
        for u in range(4):
            nc.vector.tensor_copy(b_sb[u][:, :S], b_ps[u][:])
        for c in range(1, CHUNKS):
            members(c)
            finish_z(c - 1)
        b5_first = keep.tile([P, S], F32, name="b5_first", tag="ex0")
        b_pair(0, b5_first[:])
        finish_z(CHUNKS - 1)
        b5_rest = keep.tile([P, 3, S], F32, name="b5_rest", tag="pair_b5")
        for u in range(1, 4):
            b_pair(u, b5_rest[:, u - 1, :])

        for u in range(4):
            gate = keep.tile(
                [P, CHUNKS * S if u == 0 else S + SPARE], F32, name="gate%d" % u, tag="diff_log" if u == 0 else "a_sb%d" % u
            )
            pieces = [slice(0, S)] if u < 3 else [slice(0, S - P), slice(S - P, S)]
            a4 = ring.tile([P, S], F32, name="a4", bufs=4)
            a_sum = ring.tile([P, S], F32, name="a_sum", bufs=4)
            for cols in pieces:
                fetch(a4[:, cols], a_sb[u], entries(n4_t, cols.start, cols.stop - cols.start))
                nc.vector.tensor_tensor(a_sum[:, cols], a4[:, cols], a_ps[u][:, cols], ALU.add)
            for cols in pieces:
                nc.scalar.activation(gate[:, cols], b_sum[:, u, cols], ACT.Sigmoid, scale=0.0625)
                res = ring.tile([P, S], F32, name="res", bufs=5)
                nc.vector.scalar_tensor_tensor(res[:, cols], a_sum[:, cols], 0.0625, gate[:, cols], ALU.mult, ALU.mult)
                nc.sync.dma_start(out[u * P : (u + 1) * P, cols], res[:, cols])
